import numpy as np
import ml_dtypes


def mxq(x, axis, fmt="e4m3"):
    dtype, down = {"e4m3": (ml_dtypes.float8_e4m3fn, 7), "e5m2": (ml_dtypes.float8_e5m2, 14)}[fmt]
    v = np.moveaxis(np.asarray(x, np.float32).astype(ml_dtypes.bfloat16).astype(np.float64), axis, -1)
    blocks = v.reshape(v.shape[:-1] + (-1, 32))
    amax = np.abs(blocks).max(-1, keepdims=True)
    byte = np.maximum(np.where(amax > 0, np.frexp(amax)[1] - 1 + 127, 0) - down, 1)
    scale = np.exp2(byte - 127.0)
    codes = (blocks / scale).astype(np.float32).astype(dtype).astype(np.float64)
    return np.moveaxis((codes * scale).reshape(v.shape), -1, axis)


WIDE = False


def mx_kscale(k):
    if not WIDE:
        return np.ones(k)
    levels = np.array([10, -10, 5, -5, 0])
    if k % 512:
        return np.exp2(np.random.permutation(np.resize(levels, k // 32))).repeat(32)
    a = np.empty((k // 512, 16))
    for p in range(k // 512):
        a[p, :8] = np.random.permutation(np.resize(levels, 8))
        for g in range(8):
            far = levels[np.abs(levels - a[p, g]) >= 10]
            a[p, g + 8] = far[np.random.randint(len(far))]
    return np.exp2(a.ravel()).repeat(32)


def f64(x):
    return np.asarray(x).astype(np.float64)


def striped(idx):
    return np.tile(np.asarray(idx).reshape(-1, 16).T, (8, 1)).astype(np.uint16)


def unstriped(offs):
    return offs[:16].T.reshape(-1).astype(np.int64)


E2M1 = np.array([0.0, 0.5, 1.0, 1.5, 2.0, 3.0, 4.0, 6.0, -0.0, -0.5, -1.0, -1.5, -2.0, -3.0, -4.0, -6.0])


def pack_weight(w, fmt):
    k, n = w.shape
    w = f64(np.asarray(w, np.float32).astype(ml_dtypes.bfloat16)).reshape(k // 32, 32, n)
    amax = np.abs(w).max(1)
    if fmt == "e4m3":
        byte = np.frexp(amax)[1] - 1 + 127 - 7
    else:
        mant, ex = np.frexp(amax / 6.0)
        byte = np.where(mant > 0.5, ex, ex - 1) + 127
    byte = np.clip(np.where(amax > 0, byte, 1), 1, 254)
    scaled = (w * np.exp2(127.0 - byte)[:, None, :]).reshape(k, n).astype(np.float32)
    by_word = np.ascontiguousarray(scaled.reshape(k // 512, 128, 4, n).transpose(0, 1, 3, 2))
    if fmt == "e4m3":
        words = by_word.astype(ml_dtypes.float8_e4m3fn).view(np.uint8)
    else:
        c = by_word.astype(ml_dtypes.float4_e2m1fn).view(np.uint8) & 0xF
        words = (c[..., 0::2] | (c[..., 1::2] << 4)).reshape(k // 512, 128, 2 * n)
    return np.ascontiguousarray(words), np.ascontiguousarray(byte.astype(np.uint8).reshape(k // 512, 16, n))


def unpack_weight(words, scales, fmt):
    g, _, n = scales.shape
    words = np.ascontiguousarray(words).reshape(g, 128, n, -1)
    if fmt == "e4m3":
        vals = words.view(ml_dtypes.float8_e4m3fn).astype(np.float64)
    else:
        nib = np.empty((g, 128, n, 4), np.uint8)
        nib[..., 0::2] = words & 0xF
        nib[..., 1::2] = words >> 4
        vals = E2M1[nib]
    vals = vals * np.repeat(np.exp2(scales.astype(np.float64) - 127.0), 8, axis=1)[..., None]
    return vals.transpose(0, 1, 3, 2).reshape(g * 512, n)


D, T, I, Q, V, G, M = 512, 2048, 512, 128, 16, 64, 512


def setup_inputs():
    n = np.random.standard_normal
    idx = np.random.permutation(T)[:I]
    idx2 = np.random.permutation(M)[:G]
    fd = mx_kscale(D)
    keysp = pack_weight(n((D, T)) / fd[:, None], "e2m1")
    return {
        "query": (n((D, Q)) * 1.0 / np.sqrt(D) * fd[:, None]).astype(np.float32),
        "keys_words": keysp[0],
        "keys_scales": keysp[1],
        "lam": (np.random.uniform(0.3, 0.8, (1, Q))).astype(np.float32),
        "wear": (np.random.uniform(0.0, 3.0, (Q, T))).astype(np.float32),
        "weary": (np.random.uniform(0.4, 1.5, (Q, 1))).astype(np.float32),
        "worth": np.tile(np.random.uniform(0.2, 2.0, T), (128, 1)).astype(np.float32),
        "old": (1.0 * n((Q, M))).astype(np.float32),
        "offs": striped(idx),
        "offs2": striped(idx2),
    }


def reference(query, keys_words, keys_scales, lam, wear, weary, worth, old, offs, offs2):
    idx = unstriped(offs)
    idx2 = unstriped(offs2)
    keysu = unpack_weight(keys_words, keys_scales, "e2m1")
    keysidxg = keysu[:, idx]
    queryq = mxq(f64(query), 0, "e4m3")
    a0 = keysidxg.T @ queryq
    ag = a0.reshape(I, V, Q // V).max(axis=2)
    ar = np.repeat(ag, Q // V, axis=1)
    s0 = a0 - ar * f64(lam)
    s = s0.T
    p = np.exp(s) / (f64(wear)[:, idx] * f64(weary) + 1.0)
    w = p / np.sum(p, axis=1, keepdims=True)
    ws = w * f64(worth)[:1][:, idx] * 512.0
    wp = ws.reshape(Q, G, I // G).sum(axis=2)
    wf = np.zeros((Q, M))
    wf[:, idx2] = wp
    y = f64(old) + wf
    return y

@@ -1,0 +1,159 @@
+from contextlib import ExitStack
+
+import concourse.mybir as mybir
+from concourse.masks import make_identity
+
+D, T, I, Q, V, G, M = 512, 2048, 512, 128, 16, 64, 512
+FLOPS = 2 * D * I * Q
+P = 128
+F32 = mybir.dt.float32
+BF16 = mybir.dt.bfloat16
+I32 = mybir.dt.int32
+U32 = mybir.dt.uint32
+U16 = mybir.dt.uint16
+U8 = mybir.dt.uint8
+FP8X4 = mybir.dt.float8_e4m3fn_x4
+FP4X4 = mybir.dt.float4_e2m1fn_x4
+ALU = mybir.AluOpType
+ACT = mybir.ActivationFunctionType
+AX = mybir.AxisListType
+H = I // 2
+R = Q // V
+RUN = I // G
+
+
+def tile_attend_groupbest_wornout_pagesums_kernel(tc, query, keys_words, keys_scales, lam, wear, weary, worth, old, offs, offs2, out):
+    nc = tc.nc
+    with ExitStack() as ctx:
+        sb = ctx.enter_context(tc.tile_pool(name="sb", bufs=1))
+        ps = ctx.enter_context(tc.psum_pool(name="ps", bufs=1))
+
+        offs_sb = sb.tile([P, I // 16], U16, name="offs_sb")
+        offs2_sb = sb.tile([P, G // 16], U16, name="offs2_sb")
+        words = sb.tile([P, T], U16, name="words", align_bytes=64)
+        scales = sb.tile([P, T], U8, name="scales", align_bytes=64)
+        q_raw = sb.tile([P, 4, Q], F32, name="q_raw")
+        wear_sb = sb.tile([P, T], F32, name="wear_sb")
+        worth_sb = sb.tile([P, T], F32, name="worth_sb")
+        old_sb = sb.tile([P, M], F32, name="old_sb")
+        lam_col = sb.tile([P, 1], F32, name="lam_col")
+        weary_col = sb.tile([P, 1], F32, name="weary_col")
+        ident = sb.tile([P, P], F32, name="ident")
+        placed = sb.tile([P, M], F32, name="placed")
+
+        nc.gpsimd.memset(scales[:].bitcast(I32), 0)
+        nc.gpsimd.memset(worth_sb[:, : T // 4], 0.0)
+        nc.vector.memset(worth_sb[:, T // 4 :], 0.0)
+        nc.vector.memset(placed[:], 0.0)
+
+        nc.sync.dma_start(offs_sb[:], offs)
+        nc.sync.dma_start(words[:].bitcast(I32), keys_words[0].bitcast(I32))
+        for quad in range(4):
+            nc.sync.dma_start(scales[32 * quad : 32 * quad + 4, :].bitcast(I32), keys_scales[0, 4 * quad : 4 * quad + 4, :].bitcast(I32))
+        nc.sync.dma_start(q_raw[:], query.rearrange("(p j) q -> p j q", j=4))
+        nc.sync.dma_start(wear_sb[:], wear)
+        nc.scalar.dma_start(worth_sb[0:1, :], worth[0:1, :])
+        nc.sync.dma_start(offs2_sb[:], offs2)
+        nc.sync.dma_start(old_sb[:], old)
+        with nc.allow_non_contiguous_dma(reason="one value a partition"):
+            nc.gpsimd.dma_start(weary_col[:], weary)
+            nc.gpsimd.dma_start(lam_col[:], lam.rearrange("o q -> q o"))
+        make_identity(nc, ident[:])
+
+        kw = sb.tile([P, I], U16, name="kw", align_bytes=64)
+        nc.vector.tensor_copy(kw[:], words[:].indirect(offs_sb[:]))
+        q_bf = sb.tile([P, Q, 4], BF16, name="q_bf", align_bytes=64)
+        nc.scalar.copy(q_bf[:], q_raw[:].rearrange("p j q -> p q j"))
+        q_codes = sb.tile([P, Q], U32, name="q_codes", align_bytes=64)
+        q_scales = sb.tile([P, Q], U8, name="q_scales", align_bytes=64)
+        nc.vector.quantize_mx(out=q_codes[:].bitcast(FP8X4), scales=q_scales[:], in_=q_bf[:].rearrange("p q j -> p (q j)"))
+        halves = [offs_sb[:, h * (H // 16) : (h + 1) * (H // 16)] for h in range(2)]
+        ks = [sb.tile([P, H], U8, name=f"ks{h}", align_bytes=64) for h in range(2)]
+        for h in range(2):
+            nc.vector.tensor_copy(ks[h][:], scales[:].indirect(halves[h]))
+
+        worth_g = sb.tile([P, I], F32, name="worth_g")
+        nc.scalar.activation(worth_g[:], worth_sb[:].indirect(offs_sb[:]), ACT.Copy)
+        worth_t = ps.tile([P, 4, P], F32, name="worth_t")
+        for j in range(4):
+            nc.tensor.transpose(worth_t[:, j, :], worth_g[:, j * P : (j + 1) * P], ident[:])
+        worth_col = sb.tile([P, 4], F32, name="worth_col")
+        nc.scalar.activation(worth_col[:], worth_t[:, :, 0], ACT.Copy, scale=512.0)
+        worth_rows = ps.tile([P, I], F32, name="worth_rows")
+        for j in range(4):
+            nc.tensor.transpose(worth_rows[:, j * P : (j + 1) * P], worth_col[:, j : j + 1].to_broadcast([P, P]), ident[:])
+        lam_rows = ps.tile([P, Q], F32, name="lam_rows")
+        nc.tensor.transpose(lam_rows[:], lam_col[:].to_broadcast([P, P]), ident[:])
+
+        a0 = [ps.tile([P, 2, Q], F32, name=f"a0_{h}") for h in range(2)]
+        for h in range(2):
+            for j in range(2):
+                c0 = h * H + j * P
+                nc.tensor.matmul_mx(out=a0[h][:, j, :], lhsT=kw[:, c0 : c0 + P].bitcast(FP4X4), lhsT_scale=ks[h][:, j * P : (j + 1) * P],
+                                    rhs=q_codes[:].bitcast(FP8X4), rhs_scale=q_scales[:], start=True, stop=True)
+        den = [sb.tile([P, H], F32, name=f"den{h}") for h in range(2)]
+        for h in range(2):
+            nc.scalar.activation(den[h][:], wear_sb[:].indirect(halves[h]), ACT.Copy, bias=1.0, scale=weary_col[:])
+
+        best = [sb.tile([P, 2 * V], F32, name=f"best{h}") for h in range(2)]
+        shift = [sb.tile([P, 2, Q], F32, name=f"shift{h}") for h in range(2)]
+        a0_sb = [sb.tile([P, 2, Q], F32, name=f"a0_sb{h}") for h in range(2)]
+        s_t = [ps.tile([P, H], F32, name=f"s_t{h}") for h in range(2)]
+        e = [sb.tile([P, H], F32, name=f"e{h}") for h in range(2)]
+        for h in range(2):
+            nc.vector.tensor_reduce(best[h][:], a0[h][:].rearrange("p j (v r) -> p (j v) r", r=R), AX.X, ALU.max, negate=True)
+        for h in range(2):
+            nc.vector.tensor_tensor(
+                shift[h][:].rearrange("p j (v r) -> p j v r", r=R),
+                best[h][:].rearrange("p (j v) -> p j v", j=2).unsqueeze(3).to_broadcast([P, 2, V, R]),
+                lam_rows[:].rearrange("p (v r) -> p v r", r=R).unsqueeze(1).to_broadcast([P, 2, V, R]),
+                ALU.mult)
+        for h in range(2):
+            nc.scalar.copy(a0_sb[h][:], a0[h][:])
+        for h in range(2):
+            for j in range(2):
+                o = s_t[h][:, j * P : (j + 1) * P]
+                nc.tensor.matmul(o, lhsT=shift[h][:, j, :], rhs=ident[:], start=True, stop=False, is_transpose=True)
+                nc.tensor.matmul(o, lhsT=a0_sb[h][:, j, :], rhs=ident[:], start=False, stop=True, is_transpose=True)
+        for h in range(2):
+            nc.scalar.activation(e[h][:], s_t[h][:], ACT.Exp)
+
+        p2 = [sb.tile([P, 2, H // 4], F32, name=f"p2_{h}") for h in range(2)]
+        p4 = [sb.tile([P, H // 4], F32, name=f"p4_{h}") for h in range(2)]
+        r4 = [sb.tile([P, H // 4], F32, name=f"r4_{h}") for h in range(2)]
+        r2 = [sb.tile([P, 2, H // 4], F32, name=f"r2_{h}") for h in range(2)]
+        r1 = [sb.tile([P, 2, H // 2], F32, name=f"r1_{h}") for h in range(2)]
+        for h in range(2):
+            nc.vector.tensor_tensor(p2[h][:].rearrange("p a n -> p (a n)"), den[h][:, : H // 2], den[h][:, H // 2 :], ALU.mult)
+        for h in range(2):
+            nc.vector.tensor_tensor(p4[h][:], p2[h][:, 0, :], p2[h][:, 1, :], ALU.mult)
+        for h in range(2):
+            nc.vector.reciprocal(r4[h][:], p4[h][:])
+        for h in range(2):
+            nc.vector.tensor_tensor(r2[h][:], r4[h][:].unsqueeze(1).to_broadcast([P, 2, H // 4]), p2[h][:, ::-1, :], ALU.mult)
+        for h in range(2):
+            nc.vector.tensor_tensor(r1[h][:], r2[h][:].rearrange("p a n -> p (a n)").unsqueeze(1).to_broadcast([P, 2, H // 2]),
+                                    den[h][:].rearrange("p (a n) -> p a n", a=2)[:, ::-1, :], ALU.mult)
+
+        part = [sb.tile([P, H], F32, name=f"part{h}") for h in range(2)]
+        tot = [sb.tile([P, 1], F32, name=f"tot{h}") for h in range(2)]
+        pw = [sb.tile([P, H], F32, name=f"pw{h}") for h in range(2)]
+        runs = sb.tile([P, G], F32, name="runs")
+        total = sb.tile([P, 1], F32, name="total")
+        inv = sb.tile([P, 1], F32, name="inv")
+        inv_row = sb.tile([P, G], F32, name="inv_row")
+        for h in range(2):
+            nc.vector.scalar_tensor_tensor(part[h][:], e[h][:], 1.0, r1[h][:].rearrange("p a n -> p (a n)"), ALU.mult, ALU.mult, accum_out=tot[h][:])
+        nc.vector.tensor_tensor(pw[0][:], part[0][:], worth_rows[:, :H], ALU.mult)
+        nc.vector.tensor_tensor(total[:], tot[0][:], tot[1][:], ALU.add)
+        nc.vector.tensor_tensor(pw[1][:], part[1][:], worth_rows[:, H:], ALU.mult)
+        nc.vector.reciprocal(inv[:], total[:])
+        nc.scalar.copy(inv_row[:], inv[:].to_broadcast([P, G]))
+        for h in range(2):
+            nc.vector.tensor_reduce(runs[:, h * (G // 2) : (h + 1) * (G // 2)], pw[h][:].rearrange("p (g r) -> p g r", r=RUN), AX.X, ALU.add)
+        nc.vector.tensor_tensor(placed[:].indirect(offs2_sb[:]), runs[:], inv_row[:], ALU.mult)
+        res = [sb.tile([P, M // 2], F32, name=f"res{h}") for h in range(2)]
+        for h in range(2):
+            cols = slice(h * (M // 2), (h + 1) * (M // 2))
+            nc.vector.tensor_tensor(res[h][:], placed[:, cols], old_sb[:, cols], ALU.add)
+            (nc.sync, nc.scalar)[h].dma_start(out[:, cols], res[h][:])

@@ -32,58 +32,54 @@ def tile_attend_groupbest_wornout_pagesums_kernel(tc, query, keys_words, keys_sc
         offs2_sb = sb.tile([P, G // 16], U16, name="offs2_sb")
         words = sb.tile([P, T], U16, name="words", align_bytes=64)
         scales = sb.tile([P, T], U8, name="scales", align_bytes=64)
-        q_raw = sb.tile([P, 4, Q], F32, name="q_raw")
-        wear_sb = sb.tile([P, T], F32, name="wear_sb")
+        q_raw = sb.tile([P, 4, Q], F32, name="q_raw", tag="rows")
+        wear_sb = sb.tile([P, T], F32, name="wear_sb", tag="wide")
         worth_sb = sb.tile([P, T], F32, name="worth_sb")
-        old_sb = sb.tile([P, M], F32, name="old_sb")
-        lam_col = sb.tile([P, 1], F32, name="lam_col")
+        lam_rows = sb.tile([P, Q], F32, name="lam_rows")
         weary_col = sb.tile([P, 1], F32, name="weary_col")
         ident = sb.tile([P, P], F32, name="ident")
         placed = sb.tile([P, M], F32, name="placed")
 
-        nc.gpsimd.memset(scales[:].bitcast(I32), 0)
-        nc.gpsimd.memset(worth_sb[:, : T // 4], 0.0)
-        nc.vector.memset(worth_sb[:, T // 4 :], 0.0)
+        nc.gpsimd.memset(scales[:, : T // 2].bitcast(I32), 0)
+        nc.vector.memset(scales[:, T // 2 :].bitcast(I32), 0)
+        nc.gpsimd.memset(worth_sb[: P - 1, : T // 2], 0.0)
+        nc.vector.memset(worth_sb[: P - 1, T // 2 :], 0.0)
         nc.vector.memset(placed[:], 0.0)
 
         nc.sync.dma_start(offs_sb[:], offs)
+        nc.scalar.dma_start(worth_sb[P - 1 : P, :], worth[0:1, :])
+        with nc.allow_non_contiguous_dma(reason="one value a partition"):
+            nc.scalar.dma_start(weary_col[:], weary)
         nc.sync.dma_start(words[:].bitcast(I32), keys_words[0].bitcast(I32))
+        nc.sync.dma_start(q_raw[:], query.rearrange("(p j) q -> p j q", j=4))
         for quad in range(4):
             nc.sync.dma_start(scales[32 * quad : 32 * quad + 4, :].bitcast(I32), keys_scales[0, 4 * quad : 4 * quad + 4, :].bitcast(I32))
-        nc.sync.dma_start(q_raw[:], query.rearrange("(p j) q -> p j q", j=4))
         nc.sync.dma_start(wear_sb[:], wear)
-        nc.scalar.dma_start(worth_sb[0:1, :], worth[0:1, :])
+        nc.sync.dma_start(lam_rows[:], lam[0].partition_broadcast(P))
         nc.sync.dma_start(offs2_sb[:], offs2)
-        nc.sync.dma_start(old_sb[:], old)
-        with nc.allow_non_contiguous_dma(reason="one value a partition"):
-            nc.gpsimd.dma_start(weary_col[:], weary)
-            nc.gpsimd.dma_start(lam_col[:], lam.rearrange("o q -> q o"))
         make_identity(nc, ident[:])
-
-        kw = sb.tile([P, I], U16, name="kw", align_bytes=64)
-        nc.vector.tensor_copy(kw[:], words[:].indirect(offs_sb[:]))
-        q_bf = sb.tile([P, Q, 4], BF16, name="q_bf", align_bytes=64)
-        nc.scalar.copy(q_bf[:], q_raw[:].rearrange("p j q -> p q j"))
-        q_codes = sb.tile([P, Q], U32, name="q_codes", align_bytes=64)
-        q_scales = sb.tile([P, Q], U8, name="q_scales", align_bytes=64)
-        nc.vector.quantize_mx(out=q_codes[:].bitcast(FP8X4), scales=q_scales[:], in_=q_bf[:].rearrange("p q j -> p (q j)"))
-        halves = [offs_sb[:, h * (H // 16) : (h + 1) * (H // 16)] for h in range(2)]
-        ks = [sb.tile([P, H], U8, name=f"ks{h}", align_bytes=64) for h in range(2)]
-        for h in range(2):
-            nc.vector.tensor_copy(ks[h][:], scales[:].indirect(halves[h]))
 
         worth_g = sb.tile([P, I], F32, name="worth_g")
         nc.scalar.activation(worth_g[:], worth_sb[:].indirect(offs_sb[:]), ACT.Copy)
+
+        halves = [offs_sb[:, h * (H // 16) : (h + 1) * (H // 16)] for h in range(2)]
+        kw = sb.tile([P, I], U16, name="kw", align_bytes=64)
+        nc.vector.tensor_copy(kw[:], words[:].indirect(offs_sb[:]))
+        q_bf = sb.tile([P, Q, 4], BF16, name="q_bf", tag="staged", align_bytes=64)
+        nc.scalar.copy(q_bf[:], q_raw[:].rearrange("p j q -> p q j"))
+        old_sb = sb.tile([P, M], F32, name="old_sb", tag="rows")
+        nc.sync.dma_start(old_sb[:], old)
+        q_codes = sb.tile([P, Q], U32, name="q_codes", align_bytes=64)
+        q_scales = sb.tile([P, Q], U8, name="q_scales", align_bytes=64)
+        ks = [sb.tile([P, H], U8, name="ks0", align_bytes=64)]
+        nc.vector.tensor_copy(ks[0][:], scales[:].indirect(halves[0]))
+        nc.vector.quantize_mx(out=q_codes[:].bitcast(FP8X4), scales=q_scales[:], in_=q_bf[:].rearrange("p q j -> p (q j)"))
+        ks.append(sb.tile([P, H], U8, name="ks1", tag="staged", align_bytes=64))
+        nc.vector.tensor_copy(ks[1][:], scales[:].indirect(halves[1]))
+
         worth_t = ps.tile([P, 4, P], F32, name="worth_t")
         for j in range(4):
             nc.tensor.transpose(worth_t[:, j, :], worth_g[:, j * P : (j + 1) * P], ident[:])
-        worth_col = sb.tile([P, 4], F32, name="worth_col")
-        nc.scalar.activation(worth_col[:], worth_t[:, :, 0], ACT.Copy, scale=512.0)
-        worth_rows = ps.tile([P, I], F32, name="worth_rows")
-        for j in range(4):
-            nc.tensor.transpose(worth_rows[:, j * P : (j + 1) * P], worth_col[:, j : j + 1].to_broadcast([P, P]), ident[:])
-        lam_rows = ps.tile([P, Q], F32, name="lam_rows")
-        nc.tensor.transpose(lam_rows[:], lam_col[:].to_broadcast([P, P]), ident[:])
 
         a0 = [ps.tile([P, 2, Q], F32, name=f"a0_{h}") for h in range(2)]
         for h in range(2):
@@ -91,13 +87,16 @@ def tile_attend_groupbest_wornout_pagesums_kernel(tc, query, keys_words, keys_sc
                 c0 = h * H + j * P
                 nc.tensor.matmul_mx(out=a0[h][:, j, :], lhsT=kw[:, c0 : c0 + P].bitcast(FP4X4), lhsT_scale=ks[h][:, j * P : (j + 1) * P],
                                     rhs=q_codes[:].bitcast(FP8X4), rhs_scale=q_scales[:], start=True, stop=True)
-        den = [sb.tile([P, H], F32, name=f"den{h}") for h in range(2)]
+        den_t = [sb.tile([P, H], F32, name=f"den{h}") for h in range(2)]
+        den = [t[:] for t in den_t]
         for h in range(2):
-            nc.scalar.activation(den[h][:], wear_sb[:].indirect(halves[h]), ACT.Copy, bias=1.0, scale=weary_col[:])
+            nc.scalar.activation(den[h], wear_sb[:].indirect(halves[h]), ACT.Copy, bias=1.0, scale=weary_col[:])
 
         best = [sb.tile([P, 2 * V], F32, name=f"best{h}") for h in range(2)]
         shift = [sb.tile([P, 2, Q], F32, name=f"shift{h}") for h in range(2)]
-        a0_sb = [sb.tile([P, 2, Q], F32, name=f"a0_sb{h}") for h in range(2)]
+        late = sb.tile([P, I + 8], F32, name="late", tag="wide")
+        a0_sb = [late[:, h * H : (h + 1) * H].rearrange("p (j q) -> p j q", j=2) for h in range(2)]
+        worth_col = late[:, I : I + 4]
         s_t = [ps.tile([P, H], F32, name=f"s_t{h}") for h in range(2)]
         e = [sb.tile([P, H], F32, name=f"e{h}") for h in range(2)]
         for h in range(2):
@@ -109,7 +108,7 @@ def tile_attend_groupbest_wornout_pagesums_kernel(tc, query, keys_words, keys_sc
                 lam_rows[:].rearrange("p (v r) -> p v r", r=R).unsqueeze(1).to_broadcast([P, 2, V, R]),
                 ALU.mult)
         for h in range(2):
-            nc.scalar.copy(a0_sb[h][:], a0[h][:])
+            nc.scalar.copy(a0_sb[h], a0[h][:])
         for h in range(2):
             for j in range(2):
                 o = s_t[h][:, j * P : (j + 1) * P]
@@ -117,6 +116,11 @@ def tile_attend_groupbest_wornout_pagesums_kernel(tc, query, keys_words, keys_sc
                 nc.tensor.matmul(o, lhsT=a0_sb[h][:, j, :], rhs=ident[:], start=False, stop=True, is_transpose=True)
         for h in range(2):
             nc.scalar.activation(e[h][:], s_t[h][:], ACT.Exp)
+
+        nc.scalar.activation(worth_col, worth_t[:, :, P - 1], ACT.Copy, scale=512.0)
+        worth_rows = ps.tile([P, I], F32, name="worth_rows")
+        for j in range(4):
+            nc.tensor.transpose(worth_rows[:, j * P : (j + 1) * P], worth_col[:, j : j + 1].to_broadcast([P, P]), ident[:])
 
         p2 = [sb.tile([P, 2, H // 4], F32, name=f"p2_{h}") for h in range(2)]
         p4 = [sb.tile([P, H // 4], F32, name=f"p4_{h}") for h in range(2)]
@@ -133,7 +137,7 @@ def tile_attend_groupbest_wornout_pagesums_kernel(tc, query, keys_words, keys_sc
             nc.vector.tensor_tensor(r2[h][:], r4[h][:].unsqueeze(1).to_broadcast([P, 2, H // 4]), p2[h][:, ::-1, :], ALU.mult)
         for h in range(2):
             nc.vector.tensor_tensor(r1[h][:], r2[h][:].rearrange("p a n -> p (a n)").unsqueeze(1).to_broadcast([P, 2, H // 2]),
-                                    den[h][:].rearrange("p (a n) -> p a n", a=2)[:, ::-1, :], ALU.mult)
+                                    den[h].rearrange("p (a n) -> p a n", a=2)[:, ::-1, :], ALU.mult)
 
         part = [sb.tile([P, H], F32, name=f"part{h}") for h in range(2)]
         tot = [sb.tile([P, 1], F32, name=f"tot{h}") for h in range(2)]

@@ -35,29 +35,30 @@ def tile_attend_groupbest_wornout_pagesums_kernel(tc, query, keys_words, keys_sc
         q_raw = sb.tile([P, 4, Q], F32, name="q_raw", tag="rows")
         wear_sb = sb.tile([P, T], F32, name="wear_sb", tag="wide")
         worth_sb = sb.tile([P, T], F32, name="worth_sb")
-        lam_rows = sb.tile([P, Q], F32, name="lam_rows")
+        lam_col = sb.tile([P, 1], F32, name="lam_col")
         weary_col = sb.tile([P, 1], F32, name="weary_col")
         ident = sb.tile([P, P], F32, name="ident")
         placed = sb.tile([P, M], F32, name="placed")
 
         nc.gpsimd.memset(scales[:, : T // 2].bitcast(I32), 0)
         nc.vector.memset(scales[:, T // 2 :].bitcast(I32), 0)
-        nc.gpsimd.memset(worth_sb[: P - 1, : T // 2], 0.0)
-        nc.vector.memset(worth_sb[: P - 1, T // 2 :], 0.0)
+        nc.vector.memset(worth_sb[: P - 1, :], 0.0)
         nc.vector.memset(placed[:], 0.0)
 
         nc.sync.dma_start(offs_sb[:], offs)
-        nc.scalar.dma_start(worth_sb[P - 1 : P, :], worth[0:1, :])
         with nc.allow_non_contiguous_dma(reason="one value a partition"):
+            nc.sync.dma_start(lam_col[:], lam.rearrange("o q -> q o"))
             nc.scalar.dma_start(weary_col[:], weary)
+        nc.scalar.dma_start(worth_sb[P - 1 : P, :], worth[0:1, :])
         nc.sync.dma_start(words[:].bitcast(I32), keys_words[0].bitcast(I32))
         nc.sync.dma_start(q_raw[:], query.rearrange("(p j) q -> p j q", j=4))
         for quad in range(4):
             nc.sync.dma_start(scales[32 * quad : 32 * quad + 4, :].bitcast(I32), keys_scales[0, 4 * quad : 4 * quad + 4, :].bitcast(I32))
         nc.sync.dma_start(wear_sb[:], wear)
-        nc.sync.dma_start(lam_rows[:], lam[0].partition_broadcast(P))
         nc.sync.dma_start(offs2_sb[:], offs2)
         make_identity(nc, ident[:])
+        lam_rows = ps.tile([P, Q], F32, name="lam_rows")
+        nc.tensor.transpose(lam_rows[:], lam_col[:].to_broadcast([P, P]), ident[:])
 
         worth_g = sb.tile([P, I], F32, name="worth_g")
         nc.scalar.activation(worth_g[:], worth_sb[:].indirect(offs_sb[:]), ACT.Copy)

from contextlib import ExitStack

import concourse.mybir as mybir
from concourse.masks import make_identity

D, T, I, Q, V, G, M = 512, 2048, 512, 128, 16, 64, 512
FLOPS = 2 * D * I * Q
P = 128
F32 = mybir.dt.float32
BF16 = mybir.dt.bfloat16
I32 = mybir.dt.int32
U32 = mybir.dt.uint32
U16 = mybir.dt.uint16
U8 = mybir.dt.uint8
FP8X4 = mybir.dt.float8_e4m3fn_x4
FP4X4 = mybir.dt.float4_e2m1fn_x4
ALU = mybir.AluOpType
ACT = mybir.ActivationFunctionType
AX = mybir.AxisListType
H = I // 2
R = Q // V
RUN = I // G


def tile_attend_groupbest_wornout_pagesums_kernel(tc, query, keys_words, keys_scales, lam, wear, weary, worth, old, offs, offs2, out):
    nc = tc.nc
    with ExitStack() as ctx:
        sb = ctx.enter_context(tc.tile_pool(name="sb", bufs=1))
        ps = ctx.enter_context(tc.psum_pool(name="ps", bufs=1))

        offs_sb = sb.tile([P, I // 16], U16, name="offs_sb")
        offs2_sb = sb.tile([P, G // 16], U16, name="offs2_sb")
        words = sb.tile([P, T], U16, name="words", align_bytes=64)
        scales = sb.tile([P, T], U8, name="scales", align_bytes=64)
        q_raw = sb.tile([P, 4, Q], F32, name="q_raw", tag="rows")
        wear_sb = sb.tile([P, T], F32, name="wear_sb", tag="wide")
        worth_sb = sb.tile([P, T], F32, name="worth_sb")
        lam_col = sb.tile([P, 1], F32, name="lam_col")
        weary_col = sb.tile([P, 1], F32, name="weary_col")
        ident = sb.tile([P, P], F32, name="ident")
        placed = sb.tile([P, M], F32, name="placed")

        nc.gpsimd.memset(scales[:, : T // 2].bitcast(I32), 0)
        nc.vector.memset(scales[:, T // 2 :].bitcast(I32), 0)
        nc.vector.memset(worth_sb[: P - 1, :], 0.0)
        nc.vector.memset(placed[:], 0.0)

        nc.sync.dma_start(offs_sb[:], offs)
        with nc.allow_non_contiguous_dma(reason="one value a partition"):
            nc.sync.dma_start(lam_col[:], lam.rearrange("o q -> q o"))
            nc.scalar.dma_start(weary_col[:], weary)
        nc.scalar.dma_start(worth_sb[P - 1 : P, :], worth[0:1, :])
        nc.sync.dma_start(words[:].bitcast(I32), keys_words[0].bitcast(I32))
        nc.sync.dma_start(q_raw[:], query.rearrange("(p j) q -> p j q", j=4))
        for quad in range(4):
            nc.sync.dma_start(scales[32 * quad : 32 * quad + 4, :].bitcast(I32), keys_scales[0, 4 * quad : 4 * quad + 4, :].bitcast(I32))
        nc.sync.dma_start(wear_sb[:], wear)
        nc.sync.dma_start(offs2_sb[:], offs2)
        make_identity(nc, ident[:])
        lam_rows = ps.tile([P, Q], F32, name="lam_rows")
        nc.tensor.transpose(lam_rows[:], lam_col[:].to_broadcast([P, P]), ident[:])

        worth_g = sb.tile([P, I], F32, name="worth_g")
        nc.scalar.activation(worth_g[:], worth_sb[:].indirect(offs_sb[:]), ACT.Copy)

        halves = [offs_sb[:, h * (H // 16) : (h + 1) * (H // 16)] for h in range(2)]
        kw = sb.tile([P, I], U16, name="kw", align_bytes=64)
        nc.vector.tensor_copy(kw[:], words[:].indirect(offs_sb[:]))
        q_bf = sb.tile([P, Q, 4], BF16, name="q_bf", tag="staged", align_bytes=64)
        nc.scalar.copy(q_bf[:], q_raw[:].rearrange("p j q -> p q j"))
        old_sb = sb.tile([P, M], F32, name="old_sb", tag="rows")
        nc.sync.dma_start(old_sb[:], old)
        q_codes = sb.tile([P, Q], U32, name="q_codes", align_bytes=64)
        q_scales = sb.tile([P, Q], U8, name="q_scales", align_bytes=64)
        ks = [sb.tile([P, H], U8, name="ks0", align_bytes=64)]
        nc.vector.tensor_copy(ks[0][:], scales[:].indirect(halves[0]))
        nc.vector.quantize_mx(out=q_codes[:].bitcast(FP8X4), scales=q_scales[:], in_=q_bf[:].rearrange("p q j -> p (q j)"))
        ks.append(sb.tile([P, H], U8, name="ks1", tag="staged", align_bytes=64))
        nc.vector.tensor_copy(ks[1][:], scales[:].indirect(halves[1]))

        worth_t = ps.tile([P, 4, P], F32, name="worth_t")
        for j in range(4):
            nc.tensor.transpose(worth_t[:, j, :], worth_g[:, j * P : (j + 1) * P], ident[:])

        a0 = [ps.tile([P, 2, Q], F32, name=f"a0_{h}") for h in range(2)]
        for h in range(2):
            for j in range(2):
                c0 = h * H + j * P
                nc.tensor.matmul_mx(out=a0[h][:, j, :], lhsT=kw[:, c0 : c0 + P].bitcast(FP4X4), lhsT_scale=ks[h][:, j * P : (j + 1) * P],
                                    rhs=q_codes[:].bitcast(FP8X4), rhs_scale=q_scales[:], start=True, stop=True)
        den_t = [sb.tile([P, H], F32, name=f"den{h}") for h in range(2)]
        den = [t[:] for t in den_t]
        for h in range(2):
            nc.scalar.activation(den[h], wear_sb[:].indirect(halves[h]), ACT.Copy, bias=1.0, scale=weary_col[:])

        best = [sb.tile([P, 2 * V], F32, name=f"best{h}") for h in range(2)]
        shift = [sb.tile([P, 2, Q], F32, name=f"shift{h}") for h in range(2)]
        late = sb.tile([P, I + 8], F32, name="late", tag="wide")
        a0_sb = [late[:, h * H : (h + 1) * H].rearrange("p (j q) -> p j q", j=2) for h in range(2)]
        worth_col = late[:, I : I + 4]
        s_t = [ps.tile([P, H], F32, name=f"s_t{h}") for h in range(2)]
        e = [sb.tile([P, H], F32, name=f"e{h}") for h in range(2)]
        for h in range(2):
            nc.vector.tensor_reduce(best[h][:], a0[h][:].rearrange("p j (v r) -> p (j v) r", r=R), AX.X, ALU.max, negate=True)
        for h in range(2):
            nc.vector.tensor_tensor(
                shift[h][:].rearrange("p j (v r) -> p j v r", r=R),
                best[h][:].rearrange("p (j v) -> p j v", j=2).unsqueeze(3).to_broadcast([P, 2, V, R]),
                lam_rows[:].rearrange("p (v r) -> p v r", r=R).unsqueeze(1).to_broadcast([P, 2, V, R]),
                ALU.mult)
        for h in range(2):
            nc.scalar.copy(a0_sb[h], a0[h][:])
        for h in range(2):
            for j in range(2):
                o = s_t[h][:, j * P : (j + 1) * P]
                nc.tensor.matmul(o, lhsT=shift[h][:, j, :], rhs=ident[:], start=True, stop=False, is_transpose=True)
                nc.tensor.matmul(o, lhsT=a0_sb[h][:, j, :], rhs=ident[:], start=False, stop=True, is_transpose=True)
        for h in range(2):
            nc.scalar.activation(e[h][:], s_t[h][:], ACT.Exp)

        nc.scalar.activation(worth_col, worth_t[:, :, P - 1], ACT.Copy, scale=512.0)
        worth_rows = ps.tile([P, I], F32, name="worth_rows")
        for j in range(4):
            nc.tensor.transpose(worth_rows[:, j * P : (j + 1) * P], worth_col[:, j : j + 1].to_broadcast([P, P]), ident[:])

        p2 = [sb.tile([P, 2, H // 4], F32, name=f"p2_{h}") for h in range(2)]
        p4 = [sb.tile([P, H // 4], F32, name=f"p4_{h}") for h in range(2)]
        r4 = [sb.tile([P, H // 4], F32, name=f"r4_{h}") for h in range(2)]
        r2 = [sb.tile([P, 2, H // 4], F32, name=f"r2_{h}") for h in range(2)]
        r1 = [sb.tile([P, 2, H // 2], F32, name=f"r1_{h}") for h in range(2)]
        for h in range(2):
            nc.vector.tensor_tensor(p2[h][:].rearrange("p a n -> p (a n)"), den[h][:, : H // 2], den[h][:, H // 2 :], ALU.mult)
        for h in range(2):
            nc.vector.tensor_tensor(p4[h][:], p2[h][:, 0, :], p2[h][:, 1, :], ALU.mult)
        for h in range(2):
            nc.vector.reciprocal(r4[h][:], p4[h][:])
        for h in range(2):
            nc.vector.tensor_tensor(r2[h][:], r4[h][:].unsqueeze(1).to_broadcast([P, 2, H // 4]), p2[h][:, ::-1, :], ALU.mult)
        for h in range(2):
            nc.vector.tensor_tensor(r1[h][:], r2[h][:].rearrange("p a n -> p (a n)").unsqueeze(1).to_broadcast([P, 2, H // 2]),
                                    den[h].rearrange("p (a n) -> p a n", a=2)[:, ::-1, :], ALU.mult)

        part = [sb.tile([P, H], F32, name=f"part{h}") for h in range(2)]
        tot = [sb.tile([P, 1], F32, name=f"tot{h}") for h in range(2)]
        pw = [sb.tile([P, H], F32, name=f"pw{h}") for h in range(2)]
        runs = sb.tile([P, G], F32, name="runs")
        total = sb.tile([P, 1], F32, name="total")
        inv = sb.tile([P, 1], F32, name="inv")
        inv_row = sb.tile([P, G], F32, name="inv_row")
        for h in range(2):
            nc.vector.scalar_tensor_tensor(part[h][:], e[h][:], 1.0, r1[h][:].rearrange("p a n -> p (a n)"), ALU.mult, ALU.mult, accum_out=tot[h][:])
        nc.vector.tensor_tensor(pw[0][:], part[0][:], worth_rows[:, :H], ALU.mult)
        nc.vector.tensor_tensor(total[:], tot[0][:], tot[1][:], ALU.add)
        nc.vector.tensor_tensor(pw[1][:], part[1][:], worth_rows[:, H:], ALU.mult)
        nc.vector.reciprocal(inv[:], total[:])
        nc.scalar.copy(inv_row[:], inv[:].to_broadcast([P, G]))
        for h in range(2):
            nc.vector.tensor_reduce(runs[:, h * (G // 2) : (h + 1) * (G // 2)], pw[h][:].rearrange("p (g r) -> p g r", r=RUN), AX.X, ALU.add)
        nc.vector.tensor_tensor(placed[:].indirect(offs2_sb[:]), runs[:], inv_row[:], ALU.mult)
        res = [sb.tile([P, M // 2], F32, name=f"res{h}") for h in range(2)]
        for h in range(2):
            cols = slice(h * (M // 2), (h + 1) * (M // 2))
            nc.vector.tensor_tensor(res[h][:], placed[:, cols], old_sb[:, cols], ALU.add)
            (nc.sync, nc.scalar)[h].dma_start(out[:, cols], res[h][:])
